import numpy as np
import ml_dtypes


def mxq(x, axis, fmt="e4m3"):
    dtype, down = {"e4m3": (ml_dtypes.float8_e4m3fn, 7), "e5m2": (ml_dtypes.float8_e5m2, 14)}[fmt]
    v = np.moveaxis(np.asarray(x, np.float32).astype(ml_dtypes.bfloat16).astype(np.float64), axis, -1)
    blocks = v.reshape(v.shape[:-1] + (-1, 32))
    amax = np.abs(blocks).max(-1, keepdims=True)
    byte = np.maximum(np.where(amax > 0, np.frexp(amax)[1] - 1 + 127, 0) - down, 1)
    scale = np.exp2(byte - 127.0)
    codes = (blocks / scale).astype(np.float32).astype(dtype).astype(np.float64)
    return np.moveaxis((codes * scale).reshape(v.shape), -1, axis)


WIDE = False


def mx_kscale(k):
    if not WIDE:
        return np.ones(k)
    levels = np.array([10, -10, 5, -5, 0])
    if k % 512:
        return np.exp2(np.random.permutation(np.resize(levels, k // 32))).repeat(32)
    a = np.empty((k // 512, 16))
    for p in range(k // 512):
        a[p, :8] = np.random.permutation(np.resize(levels, 8))
        for g in range(8):
            far = levels[np.abs(levels - a[p, g]) >= 10]
            a[p, g + 8] = far[np.random.randint(len(far))]
    return np.exp2(a.ravel()).repeat(32)


def f64(x):
    return np.asarray(x).astype(np.float64)


def striped(idx):
    return np.tile(idx.reshape(-1, 16).T, (8, 1)).astype(np.uint16)


def unstriped(offs):
    return offs[:16].T.reshape(-1).astype(np.int64)


E2M1 = np.array([0.0, 0.5, 1.0, 1.5, 2.0, 3.0, 4.0, 6.0, -0.0, -0.5, -1.0, -1.5, -2.0, -3.0, -4.0, -6.0])


def pack_weight(w, fmt):
    k, n = w.shape
    w = f64(np.asarray(w, np.float32).astype(ml_dtypes.bfloat16)).reshape(k // 32, 32, n)
    amax = np.abs(w).max(1)
    if fmt == "e4m3":
        byte = np.frexp(amax)[1] - 1 + 127 - 7
    else:
        mant, ex = np.frexp(amax / 6.0)
        byte = np.where(mant > 0.5, ex, ex - 1) + 127
    byte = np.clip(np.where(amax > 0, byte, 1), 1, 254)
    scaled = (w * np.exp2(127.0 - byte)[:, None, :]).reshape(k, n).astype(np.float32)
    by_word = np.ascontiguousarray(scaled.reshape(k // 512, 128, 4, n).transpose(0, 1, 3, 2))
    if fmt == "e4m3":
        words = by_word.astype(ml_dtypes.float8_e4m3fn).view(np.uint8)
    else:
        c = by_word.astype(ml_dtypes.float4_e2m1fn).view(np.uint8) & 0xF
        words = (c[..., 0::2] | (c[..., 1::2] << 4)).reshape(k // 512, 128, 2 * n)
    return np.ascontiguousarray(words), np.ascontiguousarray(byte.astype(np.uint8).reshape(k // 512, 16, n))


def unpack_weight(words, scales, fmt):
    g, _, n = scales.shape
    words = np.ascontiguousarray(words).reshape(g, 128, n, -1)
    if fmt == "e4m3":
        vals = words.view(ml_dtypes.float8_e4m3fn).astype(np.float64)
    else:
        nib = np.empty((g, 128, n, 4), np.uint8)
        nib[..., 0::2] = words & 0xF
        nib[..., 1::2] = words >> 4
        vals = E2M1[nib]
    vals = vals * np.repeat(np.exp2(scales.astype(np.float64) - 127.0), 8, axis=1)[..., None]
    return vals.transpose(0, 1, 3, 2).reshape(g * 512, n)


def relu(v):
    return np.maximum(v, 0.0)


K, L, T, Q, E, C, D = 512, 1024, 1024, 768, 6, 128, 128
H, N = 512, 512


def by_expert(wq, xq, C):
    return np.concatenate([wq[e].T @ xq[:, e * C:(e + 1) * C] for e in range(E)], axis=1)


def setup_inputs():
    n = np.random.standard_normal
    s = mx_kscale(K)
    v = mx_kscale(L)
    u = mx_kscale(H)
    slots1, slots2 = np.random.permutation(T)[:E * C], np.random.permutation(Q)[:E * D]
    x = pack_weight(n((K, T)) * s[:, None], "e4m3")
    z = pack_weight(n((L, Q)) * v[:, None], "e4m3")
    w1 = [pack_weight(m, "e2m1") for m in n((E, K, H)) / np.sqrt(K) / s[None, :, None] * u]
    w2 = [pack_weight(m, "e2m1") for m in n((E, H, N)) / np.sqrt(H) / u[None, :, None]]
    return {
        "x_words": x[0],
        "x_scales": x[1],
        "z_words": z[0],
        "z_scales": z[1],
        "w1_words": np.stack([m[0] for m in w1]),
        "w1_scales": np.stack([m[1] for m in w1]),
        "wz": (n((E, L, H)) / np.sqrt(L) / v[None, :, None] * u).astype(np.float32),
        "w2_words": np.stack([m[0] for m in w2]),
        "w2_scales": np.stack([m[1] for m in w2]),
        "gate1": (np.tile(np.random.uniform(0.2, 1.0, E * C), (128, 1))).astype(np.float32),
        "gate2": (np.tile(np.random.uniform(0.2, 1.0, E * D), (128, 1))).astype(np.float32),
        "offs": striped(slots1),
        "offs2": striped(slots2),
    }


def reference(x_words, x_scales, z_words, z_scales, w1_words, w1_scales, wz, w2_words, w2_scales, gate1, gate2, offs, offs2):
    w1 = np.stack([unpack_weight(w1_words[e], w1_scales[e], "e2m1") for e in range(E)])
    wzq = mxq(f64(wz), 1, "e4m3")
    w2 = np.stack([unpack_weight(w2_words[e], w2_scales[e], "e2m1") for e in range(E)])
    idx, idx2 = unstriped(offs), unstriped(offs2)
    xq = unpack_weight(x_words, x_scales, "e4m3")[:, idx]
    zq = unpack_weight(z_words, z_scales, "e4m3")[:, idx2]
    h = relu(by_expert(w1, xq, C))
    p = relu(by_expert(wzq, zq, D))
    out = np.zeros((N, T + Q))
    out[:, idx] = f64(gate1[:1]) * by_expert(w2, mxq(h, 0, "e4m3"), C)
    out[:, T + idx2] = f64(gate2[:1]) * by_expert(w2, mxq(p, 0, "e4m3"), D)
    return out

@@ -1,0 +1,261 @@
+from contextlib import ExitStack
+
+import concourse.mybir as mybir
+from concourse.masks import make_identity
+
+K, L, T, Q, E, C = 512, 1024, 1024, 768, 6, 128
+H, N = 512, 512
+SLOTS = E * C
+FLOPS = 2 * SLOTS * (K * H + L * H + 2 * H * N)
+
+F32 = mybir.dt.float32
+BF16 = mybir.dt.bfloat16
+I32 = mybir.dt.int32
+U32 = mybir.dt.uint32
+U16 = mybir.dt.uint16
+U8 = mybir.dt.uint8
+FP8X4 = mybir.dt.float8_e4m3fn_x4
+FP4X4 = mybir.dt.float4_e2m1fn_x4
+ACT = mybir.ActivationFunctionType
+MULT = mybir.AluOpType.mult
+
+P = 128
+PASS = 512
+Z_PASSES = L // PASS
+BLOCKS = N // P
+WINDOW = 1024
+TEXT, PATCH = 0, 1
+TB, SB, RAWB, GRB = 3, 2, 8, 3
+SPLIT, LEAD = 3,2
+ORDER = "o xw xs 00 w1s w1a o2 zw 01 w2s w2a g1 zs 10 11 w1b w2b 20 g2"
+
+
+def tile_moe_mmo_relu_kernel(
+    tc, x_words, x_scales, z_words, z_scales, w1_words, w1_scales, wz, w2_words, w2_scales, gate1, gate2, offs, offs2, out
+):
+    nc = tc.nc
+    with ExitStack() as ctx:
+        held = ctx.enter_context(tc.tile_pool(name="held", bufs=1))
+        stream = ctx.enter_context(tc.tile_pool(name="stream", bufs=1))
+        psum = ctx.enter_context(tc.psum_pool(name="psum", bufs=1))
+
+        text_list = held.tile([P, SLOTS // 16], U16, name="text_list")
+        patch_list = held.tile([P, SLOTS // 16], U16, name="patch_list")
+        x_table = held.tile([P, T], I32, name="x_table", align_bytes=64)
+        x_scale_table = held.tile([P, T], U8, name="x_scale_table", align_bytes=64)
+        z_table = held.tile([P, Q + WINDOW], I32, name="z_table", align_bytes=64)
+        z_scale_table = held.tile([P, WINDOW], U8, name="z_scale_table", align_bytes=64)
+        x_slots = held.tile([P, SLOTS], U32, name="x_slots", align_bytes=64)
+        x_slot_scales = held.tile([P, SLOTS], U8, name="x_slot_scales", align_bytes=64)
+        z_slots = held.tile([P, Z_PASSES, SLOTS], U32, name="z_slots", align_bytes=64)
+        z_slot_scales = held.tile([P, SLOTS], U8, name="z_slot_scales", align_bytes=64)
+        w1_codes = held.tile([P, E, 2 * H], U8, name="w1_codes", align_bytes=64)
+        w1_plane = held.tile([P, E, H], U8, name="w1_plane", align_bytes=64)
+        w2_codes = held.tile([P, E, 2 * N], U8, name="w2_codes", align_bytes=64)
+        w2_plane = held.tile([P, E, N], U8, name="w2_plane", align_bytes=64)
+        gates = [held.tile([P, SLOTS], F32, name="gate%d" % m) for m in (TEXT, PATCH)]
+        identity = held.tile([P, P], F32, name="identity")
+        results = [
+            [held.tile([P, width], F32, name="result%d_%d" % (m, b)) for b in range(BLOCKS)]
+            for m, width in ((TEXT, T), (PATCH, Q))
+        ]
+        lists = (text_list, patch_list)
+
+        sum_banks = [psum.tile([P, H], F32, name="sum_bank%d" % i) for i in range(2)]
+        turn_banks = [psum.tile([P, H], F32, name="turn_bank%d" % i) for i in range(2)]
+        text_banks = [psum.tile([P, H], F32, name="text_bank%d" % i) for i in range(TB)]
+        lead_bank = psum.tile([P, H], F32, name="lead_bank")
+
+        nc.vector.memset(x_scale_table[:].bitcast(I32), 0)
+        nc.gpsimd.memset(w1_plane[:].rearrange("p e n -> p (e n)").bitcast(I32), 0)
+        nc.gpsimd.memset(w2_plane[:].rearrange("p e n -> p (e n)").bitcast(I32), 0)
+        nc.vector.memset(z_scale_table[:].bitcast(I32), 0)
+        nc.vector.memset(z_table[:, Z_PASSES * Q :], 0)
+        make_identity(nc, identity[:])
+
+        def load_weight_scales(plane, scales):
+            for r in range(4):
+                nc.sync.dma_start(
+                    out=plane[r:P:32, :, :].bitcast(I32),
+                    in_=scales[:, 0, r:16:4, :].rearrange("e q n -> q e n").bitcast(I32),
+                )
+
+        def load_wz(e, s):
+            raw = stream.tile([P, 4, H], F32, name="raw", bufs=RAWB)
+            nc.sync.dma_start(out=raw[:], in_=wz[e, s * PASS : (s + 1) * PASS, :].rearrange("(p j) c -> p j c", j=4))
+            return raw
+
+        raws = {}
+
+        def load_codes(codes, words, experts):
+            nc.sync.dma_start(
+                out=codes[:, experts, :].bitcast(I32), in_=words[experts, 0].rearrange("e p n -> p e n").bitcast(I32)
+            )
+
+        def ld(what):
+            if what == "o":
+                nc.sync.dma_start(out=text_list[:], in_=offs)
+            elif what == "xw":
+                nc.sync.dma_start(out=x_table[:], in_=x_words[0].rearrange("p t d -> p (t d)").bitcast(I32))
+            elif what == "xs":
+                for r in range(4):
+                    nc.sync.dma_start(out=x_scale_table[r:P:32, :].bitcast(I32), in_=x_scales[0, r:16:4, :].bitcast(I32))
+            elif what == "o2":
+                nc.sync.dma_start(out=patch_list[:], in_=offs2)
+            elif what == "zw":
+                nc.sync.dma_start(
+                    out=z_table[:, : Z_PASSES * Q].rearrange("p (s t) -> p s t", s=Z_PASSES),
+                    in_=z_words.rearrange("s p t d -> p s (t d)").bitcast(I32),
+                )
+            elif what == "zs":
+                for q in range(4):
+                    nc.sync.dma_start(
+                        out=z_scale_table[32 * q : 32 * q + 4 * Z_PASSES, :Q].bitcast(I32),
+                        in_=z_scales[:, 4 * q : 4 * q + 4, :].bitcast(I32),
+                    )
+            elif what == "w1s":
+                load_weight_scales(w1_plane, w1_scales)
+            elif what == "w2s":
+                load_weight_scales(w2_plane, w2_scales)
+            elif what == "w1a":
+                load_codes(w1_codes, w1_words, slice(0, SPLIT))
+            elif what == "w1b":
+                load_codes(w1_codes, w1_words, slice(SPLIT, E))
+            elif what == "w2a":
+                load_codes(w2_codes, w2_words, slice(0, SPLIT))
+            elif what == "w2b":
+                load_codes(w2_codes, w2_words, slice(SPLIT, E))
+            elif what == "g1":
+                nc.sync.dma_start(out=gates[TEXT][:], in_=gate1)
+            elif what == "g2":
+                nc.sync.dma_start(out=gates[PATCH][:], in_=gate2)
+            else:
+                raws[int(what[0]), int(what[1])] = load_wz(int(what[0]), int(what[1]))
+
+        for what in ORDER.split():
+            if SPLIT < E or what not in ("w1b", "w2b"):
+                ld(what)
+
+        nc.vector.tensor_copy(x_slots[:], x_table[:].bitcast(U32).indirect(text_list[:]))
+        nc.vector.tensor_copy(x_slot_scales[:], x_scale_table[:].indirect(text_list[:]))
+        for s in range(Z_PASSES):
+            nc.vector.tensor_copy(
+                z_slots[:, s, :], z_table[:, s * Q : s * Q + WINDOW].bitcast(U32).indirect(patch_list[:])
+            )
+        nc.vector.tensor_copy(z_slot_scales[:], z_scale_table[:].indirect(patch_list[:]))
+
+        for b in range(BLOCKS):
+            nc.vector.memset(results[TEXT][b][:], 0.0)
+
+        def quantise_wz(e):
+            grouped = stream.tile([P, Z_PASSES, H, 4], BF16, name="grouped", bufs=GRB, align_bytes=64)
+            for s in range(Z_PASSES):
+                if (e, s) not in raws:
+                    raws[e, s] = load_wz(e, s)
+                nc.scalar.activation(
+                    grouped[:, s].rearrange("p (c i) j -> p c j i", i=4),
+                    raws[e, s][:].rearrange("p j (c i) -> p c j i", i=4),
+                    ACT.Copy,
+                )
+            codes = stream.tile([P, Z_PASSES * H], U32, name="wz_codes", bufs=2, align_bytes=64)
+            plane = stream.tile([P, Z_PASSES * H], U8, name="wz_plane", bufs=2, align_bytes=64)
+            nc.vector.quantize_mx(
+                out=codes[:].bitcast(FP8X4), scales=plane[:], in_=grouped[:].rearrange("p s c j -> p (s c j)")
+            )
+            return codes, plane
+
+        def first_layer(bank, modality, e):
+            slots = slice(e * C, (e + 1) * C)
+            if modality == TEXT:
+                nc.tensor.matmul_mx(
+                    out=bank[:],
+                    lhsT=x_slots[:, slots].bitcast(FP8X4),
+                    lhsT_scale=x_slot_scales[:, slots],
+                    rhs=w1_codes[:, e, :].bitcast(FP4X4),
+                    rhs_scale=w1_plane[:, e, :],
+                    start=True,
+                    stop=True,
+                )
+            else:
+                codes, plane = wz_quantised[e]
+                for s in range(Z_PASSES):
+                    cols = slice(s * H, (s + 1) * H)
+                    nc.tensor.matmul_mx(
+                        out=bank[:],
+                        lhsT=z_slots[:, s, slots].bitcast(FP8X4),
+                        lhsT_scale=z_slot_scales[4 * s :, slots],
+                        rhs=codes[:, cols].bitcast(FP8X4),
+                        rhs_scale=plane[:, cols],
+                        start=(s == 0),
+                        stop=(s == Z_PASSES - 1),
+                    )
+            rows = stream.tile([P, H], BF16, name="rows%d" % modality, bufs=2, align_bytes=64)
+            nc.scalar.activation(
+                rows[:].rearrange("s (u p d) -> s u p d", u=2, d=2),
+                bank[:].rearrange("s (p u d) -> s u p d", u=2, d=2),
+                ACT.Relu,
+            )
+            return rows
+
+        def turn_and_quantise(bank, modality, rows):
+            pairs = rows[:].bitcast(F32)
+            for u in range(2):
+                nc.tensor.transpose(bank[:, u * C : (u + 1) * C], pairs[:, u * P : (u + 1) * P], identity[:])
+            turned = stream.tile([P, 4 * C], BF16, name="turned%d" % modality, bufs=2, align_bytes=64)
+            nc.scalar.copy(
+                turned[:].bitcast(F32).rearrange("p (s u) -> p s u", u=2),
+                bank[:, : 2 * C].rearrange("p (u s) -> p s u", u=2),
+            )
+            codes = stream.tile([P, C], U32, name="hidden_codes%d" % modality, bufs=E, align_bytes=64)
+            plane = stream.tile([P, C], U8, name="hidden_plane%d" % modality, bufs=E, align_bytes=64)
+            nc.vector.quantize_mx(out=codes[:].bitcast(FP8X4), scales=plane[:], in_=turned[:])
+            return codes, plane
+
+        def second_layer(bank, modality, e, hidden):
+            codes, plane = hidden
+            for b in range(BLOCKS):
+                nc.tensor.matmul_mx(
+                    out=bank[:, b * C : (b + 1) * C],
+                    lhsT=w2_codes[:, e, 2 * b * P : 2 * (b + 1) * P].bitcast(FP4X4),
+                    lhsT_scale=w2_plane[:, e, b * P : (b + 1) * P],
+                    rhs=codes[:].bitcast(FP8X4),
+                    rhs_scale=plane[:],
+                    start=True,
+                    stop=True,
+                )
+            sums = stream.tile([P, BLOCKS * C], F32, name="sums%d" % modality, bufs=SB)
+            nc.scalar.copy(sums[:], bank[:])
+            offsets = lists[modality][:, e * C // 16 : (e + 1) * C // 16]
+            for b in range(BLOCKS):
+                nc.vector.tensor_tensor(
+                    results[modality][b][:].indirect(offsets),
+                    sums[:, b * C : (b + 1) * C],
+                    gates[modality][:, e * C : (e + 1) * C],
+                    MULT,
+                )
+                if e == E - 1:
+                    first = modality * T
+                    width = (T, Q)[modality]
+                    nc.sync.dma_start(out=out[b * P : (b + 1) * P, first : first + width], in_=results[modality][b][:])
+
+        def text_hidden(e):
+            bank = text_banks[e % TB]
+            return turn_and_quantise(bank, TEXT, first_layer(bank, TEXT, e))
+
+        text = [text_hidden(e) for e in range(LEAD)]
+        for e in range(LEAD):
+            second_layer(text_banks[e % TB], TEXT, e, text[e])
+        wz_quantised = [quantise_wz(0)]
+        patch = []
+        for e in range(E):
+            if e + LEAD < E:
+                text.append(text_hidden(e + LEAD))
+            rows = first_layer(sum_banks[e % 2], PATCH, e)
+            if e + 1 < E:
+                wz_quantised.append(quantise_wz(e + 1))
+            patch.append(turn_and_quantise(turn_banks[e % 2], PATCH, rows))
+            if e > 0:
+                second_layer(sum_banks[e % 2], PATCH, e - 1, patch[e - 1])
+            if e + LEAD < E:
+                second_layer(turn_banks[e % 2], TEXT, e + LEAD, text[e + LEAD])
+        second_layer(lead_bank, PATCH, E - 1, patch[E - 1])

@@ -25,9 +25,9 @@ Z_PASSES = L // PASS
 BLOCKS = N // P
 WINDOW = 1024
 TEXT, PATCH = 0, 1
-TB, SB, RAWB, GRB = 3, 2, 8, 3
-SPLIT, LEAD = 3,2
-ORDER = "o xw xs 00 w1s w1a o2 zw 01 w2s w2a g1 zs 10 11 w1b w2b 20 g2"
+TB, SB, RAWB, GRB, AHEAD, VZ = 3, 2, 8, 3, 1, 2
+SPLIT, SPLIT2, GS, LEAD = 3,2,1,3
+ORDER = "o xw xs o2 zw w1s w1a 00 zs w2s w2a g1a 01 10 w1b g1b 11 w2b 20 g2"
 
 
 def tile_moe_mmo_relu_kernel(
@@ -122,19 +122,22 @@ def tile_moe_mmo_relu_kernel(
             elif what == "w1b":
                 load_codes(w1_codes, w1_words, slice(SPLIT, E))
             elif what == "w2a":
-                load_codes(w2_codes, w2_words, slice(0, SPLIT))
+                load_codes(w2_codes, w2_words, slice(0, SPLIT2))
             elif what == "w2b":
-                load_codes(w2_codes, w2_words, slice(SPLIT, E))
+                load_codes(w2_codes, w2_words, slice(SPLIT2, E))
             elif what == "g1":
                 nc.sync.dma_start(out=gates[TEXT][:], in_=gate1)
+            elif what == "g1a":
+                nc.sync.dma_start(out=gates[TEXT][:, : GS * C], in_=gate1[:, : GS * C])
+            elif what == "g1b":
+                nc.sync.dma_start(out=gates[TEXT][:, GS * C :], in_=gate1[:, GS * C :])
             elif what == "g2":
                 nc.sync.dma_start(out=gates[PATCH][:], in_=gate2)
             else:
                 raws[int(what[0]), int(what[1])] = load_wz(int(what[0]), int(what[1]))
 
         for what in ORDER.split():
-            if SPLIT < E or what not in ("w1b", "w2b"):
-                ld(what)
+            ld(what)
 
         nc.vector.tensor_copy(x_slots[:], x_table[:].bitcast(U32).indirect(text_list[:]))
         nc.vector.tensor_copy(x_slot_scales[:], x_scale_table[:].indirect(text_list[:]))
@@ -145,7 +148,10 @@ def tile_moe_mmo_relu_kernel(
         nc.vector.tensor_copy(z_slot_scales[:], z_scale_table[:].indirect(patch_list[:]))
 
         for b in range(BLOCKS):
-            nc.vector.memset(results[TEXT][b][:], 0.0)
+            if b < VZ:
+                nc.vector.memset(results[TEXT][b][:], 0.0)
+            else:
+                nc.scalar.copy(results[TEXT][b][:], results[TEXT][0][:])
 
         def quantise_wz(e):
             grouped = stream.tile([P, Z_PASSES, H, 4], BF16, name="grouped", bufs=GRB, align_bytes=64)
@@ -157,8 +163,8 @@ def tile_moe_mmo_relu_kernel(
                     raws[e, s][:].rearrange("p j (c i) -> p c j i", i=4),
                     ACT.Copy,
                 )
-            codes = stream.tile([P, Z_PASSES * H], U32, name="wz_codes", bufs=2, align_bytes=64)
-            plane = stream.tile([P, Z_PASSES * H], U8, name="wz_plane", bufs=2, align_bytes=64)
+            codes = stream.tile([P, Z_PASSES * H], U32, name="wz_codes", bufs=AHEAD + 1, align_bytes=64)
+            plane = stream.tile([P, Z_PASSES * H], U8, name="wz_plane", bufs=AHEAD + 1, align_bytes=64)
             nc.vector.quantize_mx(
                 out=codes[:].bitcast(FP8X4), scales=plane[:], in_=grouped[:].rearrange("p s c j -> p (s c j)")
             )
@@ -245,14 +251,14 @@ def tile_moe_mmo_relu_kernel(
         text = [text_hidden(e) for e in range(LEAD)]
         for e in range(LEAD):
             second_layer(text_banks[e % TB], TEXT, e, text[e])
-        wz_quantised = [quantise_wz(0)]
+        wz_quantised = [quantise_wz(e) for e in range(AHEAD)]
         patch = []
         for e in range(E):
             if e + LEAD < E:
                 text.append(text_hidden(e + LEAD))
             rows = first_layer(sum_banks[e % 2], PATCH, e)
-            if e + 1 < E:
-                wz_quantised.append(quantise_wz(e + 1))
+            if e + AHEAD < E:
+                wz_quantised.append(quantise_wz(e + AHEAD))
             patch.append(turn_and_quantise(turn_banks[e % 2], PATCH, rows))
             if e > 0:
                 second_layer(sum_banks[e % 2], PATCH, e - 1, patch[e - 1])

@@ -25,9 +25,17 @@ Z_PASSES = L // PASS
 BLOCKS = N // P
 WINDOW = 1024
 TEXT, PATCH = 0, 1
-TB, SB, RAWB, GRB, AHEAD, VZ = 3, 2, 8, 3, 1, 2
-SPLIT, SPLIT2, GS, LEAD = 3,2,1,3
-ORDER = "o xw xs o2 zw w1s w1a 00 zs w2s w2a g1a 01 10 w1b g1b 11 w2b 20 g2"
+PLANE_V = 1
+RAWB = 12
+GRB = 3
+QB = 3
+SB = 2
+TNB = 4
+HB = 3
+VZ = 1
+XCUT = ((0, 6),)
+ORDER = "o xw xs w1s o2 z0 a03 z1 zs w2s b01 g03 a36 b13 00 b36 01 g36 10 11 20 21 h06 30 31 40 41 50 51"
+PROGRAM = "Z f000 t000 f101 t101 f202 t202 s30004 f003 t003 s40104 f104 t104 f205 t205 c00 s30204@00 c01 q002 s40304@01 c10 s30404@013 c11 q102 p50@10 s40504@10 c20 c21 q202 p61@20 s31004@20 c30 c31 q302 p52@30 s41104@30 c40 p63@31 s31204@31 c41 q402 s41304@40 c50 q501 p54@41 c51 q512 s31402@50 p65@40 s61424@50 s41504"
 
 
 def tile_moe_mmo_relu_kernel(
@@ -43,7 +51,7 @@ def tile_moe_mmo_relu_kernel(
         patch_list = held.tile([P, SLOTS // 16], U16, name="patch_list")
         x_table = held.tile([P, T], I32, name="x_table", align_bytes=64)
         x_scale_table = held.tile([P, T], U8, name="x_scale_table", align_bytes=64)
-        z_table = held.tile([P, Q + WINDOW], I32, name="z_table", align_bytes=64)
+        z_tables = [held.tile([P, WINDOW], I32, name="z_table%d" % s, align_bytes=64) for s in range(Z_PASSES)]
         z_scale_table = held.tile([P, WINDOW], U8, name="z_scale_table", align_bytes=64)
         x_slots = held.tile([P, SLOTS], U32, name="x_slots", align_bytes=64)
         x_slot_scales = held.tile([P, SLOTS], U8, name="x_slot_scales", align_bytes=64)
@@ -60,32 +68,30 @@ def tile_moe_mmo_relu_kernel(
             for m, width in ((TEXT, T), (PATCH, Q))
         ]
         lists = (text_list, patch_list)
+        banks = [psum.tile([P, H], F32, name="bank%d" % i) for i in range(8)]
 
-        sum_banks = [psum.tile([P, H], F32, name="sum_bank%d" % i) for i in range(2)]
-        turn_banks = [psum.tile([P, H], F32, name="turn_bank%d" % i) for i in range(2)]
-        text_banks = [psum.tile([P, H], F32, name="text_bank%d" % i) for i in range(TB)]
-        lead_bank = psum.tile([P, H], F32, name="lead_bank")
-
+        plane_engine = nc.vector if PLANE_V else nc.gpsimd
         nc.vector.memset(x_scale_table[:].bitcast(I32), 0)
-        nc.gpsimd.memset(w1_plane[:].rearrange("p e n -> p (e n)").bitcast(I32), 0)
-        nc.gpsimd.memset(w2_plane[:].rearrange("p e n -> p (e n)").bitcast(I32), 0)
+        plane_engine.memset(w1_plane[:].rearrange("p e n -> p (e n)").bitcast(I32), 0)
         nc.vector.memset(z_scale_table[:].bitcast(I32), 0)
-        nc.vector.memset(z_table[:, Z_PASSES * Q :], 0)
+        plane_engine.memset(w2_plane[:].rearrange("p e n -> p (e n)").bitcast(I32), 0)
+        for s in range(Z_PASSES):
+            nc.vector.memset(z_tables[s][:, Q:], 0)
         make_identity(nc, identity[:])
 
-        def load_weight_scales(plane, scales):
+        def load_weight_scales(plane, scales, experts):
             for r in range(4):
                 nc.sync.dma_start(
-                    out=plane[r:P:32, :, :].bitcast(I32),
-                    in_=scales[:, 0, r:16:4, :].rearrange("e q n -> q e n").bitcast(I32),
+                    out=plane[r:P:32, experts, :].bitcast(I32),
+                    in_=scales[experts, 0, r:16:4, :].rearrange("e q n -> q e n").bitcast(I32),
                 )
 
-        def load_wz(e, s):
-            raw = stream.tile([P, 4, H], F32, name="raw", bufs=RAWB)
-            nc.sync.dma_start(out=raw[:], in_=wz[e, s * PASS : (s + 1) * PASS, :].rearrange("(p j) c -> p j c", j=4))
-            return raw
-
         raws = {}
+
+        def load_wz(e, s):
+            raw = stream.tile([P, 4 * H], F32, name="raw", bufs=RAWB, align_bytes=64)
+            nc.sync.dma_start(out=raw[:], in_=wz[e, s * PASS : (s + 1) * PASS, :].rearrange("(p j) c -> p (j c)", j=4))
+            raws[e, s] = raw
 
         def load_codes(codes, words, experts):
             nc.sync.dma_start(
@@ -102,11 +108,9 @@ def tile_moe_mmo_relu_kernel(
                     nc.sync.dma_start(out=x_scale_table[r:P:32, :].bitcast(I32), in_=x_scales[0, r:16:4, :].bitcast(I32))
             elif what == "o2":
                 nc.sync.dma_start(out=patch_list[:], in_=offs2)
-            elif what == "zw":
-                nc.sync.dma_start(
-                    out=z_table[:, : Z_PASSES * Q].rearrange("p (s t) -> p s t", s=Z_PASSES),
-                    in_=z_words.rearrange("s p t d -> p s (t d)").bitcast(I32),
-                )
+            elif what in ("z0", "z1"):
+                s = int(what[1])
+                nc.sync.dma_start(out=z_tables[s][:, :Q], in_=z_words[s].rearrange("p t d -> p (t d)").bitcast(I32))
             elif what == "zs":
                 for q in range(4):
                     nc.sync.dma_start(
@@ -114,38 +118,38 @@ def tile_moe_mmo_relu_kernel(
                         in_=z_scales[:, 4 * q : 4 * q + 4, :].bitcast(I32),
                     )
             elif what == "w1s":
-                load_weight_scales(w1_plane, w1_scales)
+                load_weight_scales(w1_plane, w1_scales, slice(0, E))
+            elif what[0] == "A":
+                load_weight_scales(w1_plane, w1_scales, slice(int(what[1]), int(what[2])))
+            elif what[0] == "B":
+                load_weight_scales(w2_plane, w2_scales, slice(int(what[1]), int(what[2])))
             elif what == "w2s":
-                load_weight_scales(w2_plane, w2_scales)
-            elif what == "w1a":
-                load_codes(w1_codes, w1_words, slice(0, SPLIT))
-            elif what == "w1b":
-                load_codes(w1_codes, w1_words, slice(SPLIT, E))
-            elif what == "w2a":
-                load_codes(w2_codes, w2_words, slice(0, SPLIT2))
-            elif what == "w2b":
-                load_codes(w2_codes, w2_words, slice(SPLIT2, E))
-            elif what == "g1":
-                nc.sync.dma_start(out=gates[TEXT][:], in_=gate1)
-            elif what == "g1a":
-                nc.sync.dma_start(out=gates[TEXT][:, : GS * C], in_=gate1[:, : GS * C])
-            elif what == "g1b":
-                nc.sync.dma_start(out=gates[TEXT][:, GS * C :], in_=gate1[:, GS * C :])
-            elif what == "g2":
-                nc.sync.dma_start(out=gates[PATCH][:], in_=gate2)
+                load_weight_scales(w2_plane, w2_scales, slice(0, E))
+            elif what[0] == "a":
+                load_codes(w1_codes, w1_words, slice(int(what[1]), int(what[2])))
+            elif what[0] == "b":
+                load_codes(w2_codes, w2_words, slice(int(what[1]), int(what[2])))
+            elif what[0] == "g":
+                cols = slice(int(what[1]) * C, int(what[2]) * C)
+                nc.sync.dma_start(out=gates[TEXT][:, cols], in_=gate1[:, cols])
+            elif what[0] == "h":
+                cols = slice(int(what[1]) * C, int(what[2]) * C)
+                nc.sync.dma_start(out=gates[PATCH][:, cols], in_=gate2[:, cols])
             else:
-                raws[int(what[0]), int(what[1])] = load_wz(int(what[0]), int(what[1]))
+                load_wz(int(what[0]), int(what[1]))
 
         for what in ORDER.split():
             ld(what)
 
-        nc.vector.tensor_copy(x_slots[:], x_table[:].bitcast(U32).indirect(text_list[:]))
-        nc.vector.tensor_copy(x_slot_scales[:], x_scale_table[:].indirect(text_list[:]))
-        for s in range(Z_PASSES):
-            nc.vector.tensor_copy(
-                z_slots[:, s, :], z_table[:, s * Q : s * Q + WINDOW].bitcast(U32).indirect(patch_list[:])
-            )
-        nc.vector.tensor_copy(z_slot_scales[:], z_scale_table[:].indirect(patch_list[:]))
+        for lo, hi in XCUT:
+            offsets = text_list[:, lo * C // 16 : hi * C // 16]
+            nc.vector.tensor_copy(x_slots[:, lo * C : hi * C], x_table[:].bitcast(U32).indirect(offsets))
+            nc.vector.tensor_copy(x_slot_scales[:, lo * C : hi * C], x_scale_table[:].indirect(offsets))
+
+        def gather_patches():
+            for s in range(Z_PASSES):
+                nc.vector.tensor_copy(z_slots[:, s, :], z_tables[s][:].bitcast(U32).indirect(patch_list[:]))
+            nc.vector.tensor_copy(z_slot_scales[:], z_scale_table[:].indirect(patch_list[:]))
 
         for b in range(BLOCKS):
             if b < VZ:
@@ -153,22 +157,36 @@ def tile_moe_mmo_relu_kernel(
             else:
                 nc.scalar.copy(results[TEXT][b][:], results[TEXT][0][:])
 
-        def quantise_wz(e):
-            grouped = stream.tile([P, Z_PASSES, H, 4], BF16, name="grouped", bufs=GRB, align_bytes=64)
-            for s in range(Z_PASSES):
-                if (e, s) not in raws:
-                    raws[e, s] = load_wz(e, s)
-                nc.scalar.activation(
-                    grouped[:, s].rearrange("p (c i) j -> p c j i", i=4),
-                    raws[e, s][:].rearrange("p j (c i) -> p c j i", i=4),
-                    ACT.Copy,
-                )
-            codes = stream.tile([P, Z_PASSES * H], U32, name="wz_codes", bufs=AHEAD + 1, align_bytes=64)
-            plane = stream.tile([P, Z_PASSES * H], U8, name="wz_plane", bufs=AHEAD + 1, align_bytes=64)
-            nc.vector.quantize_mx(
-                out=codes[:].bitcast(FP8X4), scales=plane[:], in_=grouped[:].rearrange("p s c j -> p (s c j)")
+        casted = {}
+        wz_quantised = {}
+        rows_of = {}
+        hidden = {}
+        sums_of = {}
+
+        def cast(e, s):
+            if s == 0:
+                casted[e] = stream.tile([P, Z_PASSES, H, 4], BF16, name="grouped", bufs=GRB, align_bytes=64)
+            if (e, s) not in raws:
+                load_wz(e, s)
+            nc.scalar.activation(
+                casted[e][:, s].rearrange("p (t m) j -> p m j t", t=4),
+                raws[e, s][:].rearrange("p (j m t) -> p m j t", j=4, t=4),
+                ACT.Copy,
             )
-            return codes, plane
+
+        def quantise_wz(e, passes):
+            if passes.start == 0:
+                wz_quantised[e] = (
+                    stream.tile([P, Z_PASSES * H], U32, name="wz_codes", bufs=QB, align_bytes=64),
+                    stream.tile([P, Z_PASSES * H], U8, name="wz_plane", bufs=QB, align_bytes=64),
+                )
+            codes, plane = wz_quantised[e]
+            cols = slice(passes.start * H, passes.stop * H)
+            nc.vector.quantize_mx(
+                out=codes[:, cols].bitcast(FP8X4),
+                scales=plane[:, cols],
+                in_=casted[e][:, passes].rearrange("p s c j -> p (s c j)"),
+            )
 
         def first_layer(bank, modality, e):
             slots = slice(e * C, (e + 1) * C)
@@ -201,13 +219,39 @@ def tile_moe_mmo_relu_kernel(
                 bank[:].rearrange("s (p u d) -> s u p d", u=2, d=2),
                 ACT.Relu,
             )
-            return rows
+            rows_of[modality, e] = rows
 
-        def turn_and_quantise(bank, modality, rows):
-            pairs = rows[:].bitcast(F32)
+        def patch_hidden(bank, e, room):
+            slots = slice(e * C, (e + 1) * C)
+            codes, plane = wz_quantised[e]
+            for t in range(4):
+                for s in range(Z_PASSES):
+                    cols = slice(s * H + t * P, s * H + (t + 1) * P)
+                    nc.tensor.matmul_mx(
+                        out=bank[:, t * C : (t + 1) * C],
+                        lhsT=codes[:, cols].bitcast(FP8X4),
+                        lhsT_scale=plane[:, cols],
+                        rhs=z_slots[:, s, slots].bitcast(FP8X4),
+                        rhs_scale=z_slot_scales[4 * s :, slots],
+                        start=(s == 0),
+                        stop=(s == Z_PASSES - 1),
+                    )
+            if room is None:
+                room = stream.tile([P, 4 * H], F32, name="room", bufs=2, align_bytes=64)
+            values = room[:, : 2 * C].bitcast(BF16)
+            nc.scalar.activation(
+                values.rearrange("p (c t) -> p c t", t=4), bank[:].rearrange("p (t c) -> p c t", t=4), ACT.Relu
+            )
+            codes = stream.tile([P, C], U32, name="hidden_codes1", bufs=HB, align_bytes=64)
+            plane = stream.tile([P, C], U8, name="hidden_plane1", bufs=HB, align_bytes=64)
+            nc.vector.quantize_mx(out=codes[:].bitcast(FP8X4), scales=plane[:], in_=values)
+            hidden[PATCH, e] = (codes, plane)
+
+        def turn(bank, modality, e):
+            pairs = rows_of[modality, e][:].bitcast(F32)
             for u in range(2):
                 nc.tensor.transpose(bank[:, u * C : (u + 1) * C], pairs[:, u * P : (u + 1) * P], identity[:])
-            turned = stream.tile([P, 4 * C], BF16, name="turned%d" % modality, bufs=2, align_bytes=64)
+            turned = stream.tile([P, 4 * C], BF16, name="turned%d" % modality, bufs=TNB, align_bytes=64)
             nc.scalar.copy(
                 turned[:].bitcast(F32).rearrange("p (s u) -> p s u", u=2),
                 bank[:, : 2 * C].rearrange("p (u s) -> p s u", u=2),
@@ -215,11 +259,11 @@ def tile_moe_mmo_relu_kernel(
             codes = stream.tile([P, C], U32, name="hidden_codes%d" % modality, bufs=E, align_bytes=64)
             plane = stream.tile([P, C], U8, name="hidden_plane%d" % modality, bufs=E, align_bytes=64)
             nc.vector.quantize_mx(out=codes[:].bitcast(FP8X4), scales=plane[:], in_=turned[:])
-            return codes, plane
+            hidden[modality, e] = (codes, plane)
 
-        def second_layer(bank, modality, e, hidden):
-            codes, plane = hidden
-            for b in range(BLOCKS):
+        def second_layer(bank, modality, e, blocks, room, part):
+            codes, plane = hidden[modality, e]
+            for b in blocks:
                 nc.tensor.matmul_mx(
                     out=bank[:, b * C : (b + 1) * C],
                     lhsT=w2_codes[:, e, 2 * b * P : 2 * (b + 1) * P].bitcast(FP4X4),
@@ -229,10 +273,15 @@ def tile_moe_mmo_relu_kernel(
                     start=True,
                     stop=True,
                 )
-            sums = stream.tile([P, BLOCKS * C], F32, name="sums%d" % modality, bufs=SB)
-            nc.scalar.copy(sums[:], bank[:])
+            if room is None:
+                room = stream.tile([P, BLOCKS * C], F32, name="sums", bufs=SB)
+                sums = room[:]
+            else:
+                sums = room[:, part * H : (part + 1) * H]
+            cols = slice(blocks.start * C, blocks.stop * C)
+            nc.scalar.copy(sums[:, cols], bank[:, cols])
             offsets = lists[modality][:, e * C // 16 : (e + 1) * C // 16]
-            for b in range(BLOCKS):
+            for b in blocks:
                 nc.vector.tensor_tensor(
                     results[modality][b][:].indirect(offsets),
                     sums[:, b * C : (b + 1) * C],
@@ -244,24 +293,21 @@ def tile_moe_mmo_relu_kernel(
                     width = (T, Q)[modality]
                     nc.sync.dma_start(out=out[b * P : (b + 1) * P, first : first + width], in_=results[modality][b][:])
 
-        def text_hidden(e):
-            bank = text_banks[e % TB]
-            return turn_and_quantise(bank, TEXT, first_layer(bank, TEXT, e))
-
-        text = [text_hidden(e) for e in range(LEAD)]
-        for e in range(LEAD):
-            second_layer(text_banks[e % TB], TEXT, e, text[e])
-        wz_quantised = [quantise_wz(e) for e in range(AHEAD)]
-        patch = []
-        for e in range(E):
-            if e + LEAD < E:
-                text.append(text_hidden(e + LEAD))
-            rows = first_layer(sum_banks[e % 2], PATCH, e)
-            if e + AHEAD < E:
-                wz_quantised.append(quantise_wz(e + AHEAD))
-            patch.append(turn_and_quantise(turn_banks[e % 2], PATCH, rows))
-            if e > 0:
-                second_layer(sum_banks[e % 2], PATCH, e - 1, patch[e - 1])
-            if e + LEAD < E:
-                second_layer(turn_banks[e % 2], TEXT, e + LEAD, text[e + LEAD])
-        second_layer(lead_bank, PATCH, E - 1, patch[E - 1])
+        for step in PROGRAM.split():
+            parts = step.split("@")
+            room = raws[int(parts[1][0]), int(parts[1][1])] if len(parts) > 1 else None
+            kind, args = step[0], [int(c) for c in parts[0][1:]]
+            if kind == "Z":
+                gather_patches()
+            elif kind == "c":
+                cast(args[0], args[1])
+            elif kind == "q":
+                quantise_wz(args[0], slice(args[1], args[2]))
+            elif kind == "f":
+                first_layer(banks[args[0]], args[1], args[2])
+            elif kind == "t":
+                turn(banks[args[0]], args[1], args[2])
+            elif kind == "p":
+                patch_hidden(banks[args[0]], args[1], room)
+            elif kind == "s":
+                second_layer(banks[args[0]], args[1], args[2], range(args[3], args[4]), room, int(parts[1][2]) if len(parts) > 1 and len(parts[1]) > 2 else 1 + args[1])

@@ -20,22 +20,14 @@ ACT = mybir.ActivationFunctionType
 MULT = mybir.AluOpType.mult
 
 P = 128
-PASS = 512
+PACK = 4
+PASS = P * PACK
 Z_PASSES = L // PASS
 BLOCKS = N // P
-WINDOW = 1024
+LIST_COLS = C // 16
+Z_WINDOW = 1024
+EARLY = 3
 TEXT, PATCH = 0, 1
-PLANE_V = 1
-RAWB = 12
-GRB = 3
-QB = 3
-SB = 2
-TNB = 4
-HB = 3
-VZ = 1
-XCUT = ((0, 6),)
-ORDER = "o xw xs w1s o2 z0 a03 z1 zs w2s b01 g03 a36 b13 00 b36 01 g36 10 11 20 21 h06 30 31 40 41 50 51"
-PROGRAM = "Z f000 t000 f101 t101 f202 t202 s30004 f003 t003 s40104 f104 t104 f205 t205 c00 s30204@00 c01 q002 s40304@01 c10 s30404@013 c11 q102 p50@10 s40504@10 c20 c21 q202 p61@20 s31004@20 c30 c31 q302 p52@30 s41104@30 c40 p63@31 s31204@31 c41 q402 s41304@40 c50 q501 p54@41 c51 q512 s31402@50 p65@40 s61424@50 s41504"
 
 
 def tile_moe_mmo_relu_kernel(
@@ -51,8 +43,8 @@ def tile_moe_mmo_relu_kernel(
         patch_list = held.tile([P, SLOTS // 16], U16, name="patch_list")
         x_table = held.tile([P, T], I32, name="x_table", align_bytes=64)
         x_scale_table = held.tile([P, T], U8, name="x_scale_table", align_bytes=64)
-        z_tables = [held.tile([P, WINDOW], I32, name="z_table%d" % s, align_bytes=64) for s in range(Z_PASSES)]
-        z_scale_table = held.tile([P, WINDOW], U8, name="z_scale_table", align_bytes=64)
+        z_tables = [held.tile([P, Z_WINDOW], I32, name="z_table%d" % s, align_bytes=64) for s in range(Z_PASSES)]
+        z_scale_table = held.tile([P, Z_WINDOW], U8, name="z_scale_table", align_bytes=64)
         x_slots = held.tile([P, SLOTS], U32, name="x_slots", align_bytes=64)
         x_slot_scales = held.tile([P, SLOTS], U8, name="x_slot_scales", align_bytes=64)
         z_slots = held.tile([P, Z_PASSES, SLOTS], U32, name="z_slots", align_bytes=64)
@@ -68,163 +60,151 @@ def tile_moe_mmo_relu_kernel(
             for m, width in ((TEXT, T), (PATCH, Q))
         ]
         lists = (text_list, patch_list)
-        banks = [psum.tile([P, H], F32, name="bank%d" % i) for i in range(8)]
 
-        plane_engine = nc.vector if PLANE_V else nc.gpsimd
+        text_banks = [psum.tile([P, H], F32, name="text_bank%d" % i) for i in range(3)]
+        result_banks = [psum.tile([P, BLOCKS * C], F32, name="result_bank%d" % i) for i in range(2)]
+        patch_banks = [psum.tile([P, PACK * C], F32, name="patch_bank%d" % i) for i in range(2)]
+
         nc.vector.memset(x_scale_table[:].bitcast(I32), 0)
-        plane_engine.memset(w1_plane[:].rearrange("p e n -> p (e n)").bitcast(I32), 0)
+        nc.vector.memset(w1_plane[:].rearrange("p e n -> p (e n)").bitcast(I32), 0)
         nc.vector.memset(z_scale_table[:].bitcast(I32), 0)
-        plane_engine.memset(w2_plane[:].rearrange("p e n -> p (e n)").bitcast(I32), 0)
+        nc.vector.memset(w2_plane[:].rearrange("p e n -> p (e n)").bitcast(I32), 0)
         for s in range(Z_PASSES):
             nc.vector.memset(z_tables[s][:, Q:], 0)
         make_identity(nc, identity[:])
 
-        def load_weight_scales(plane, scales, experts):
+        def load_weight_scales(plane, scales):
             for r in range(4):
                 nc.sync.dma_start(
-                    out=plane[r:P:32, experts, :].bitcast(I32),
-                    in_=scales[experts, 0, r:16:4, :].rearrange("e q n -> q e n").bitcast(I32),
+                    out=plane[r:P:32, :, :].bitcast(I32),
+                    in_=scales[:, 0, r:16:4, :].rearrange("e q n -> q e n").bitcast(I32),
                 )
 
-        raws = {}
+        def load_weight_codes(codes, words, first, last):
+            nc.sync.dma_start(
+                out=codes[:, first:last, :].bitcast(I32),
+                in_=words[first:last, 0].rearrange("e p n -> p e n").bitcast(I32),
+            )
+
+        def load_patch_words(s):
+            nc.sync.dma_start(out=z_tables[s][:, :Q], in_=z_words[s].rearrange("p t d -> p (t d)").bitcast(I32))
+
+        def load_gates(modality, first, last):
+            cols = slice(first * C, last * C)
+            nc.sync.dma_start(out=gates[modality][:, cols], in_=(gate1, gate2)[modality][:, cols])
+
+        wz_raw = {}
 
         def load_wz(e, s):
-            raw = stream.tile([P, 4 * H], F32, name="raw", bufs=RAWB, align_bytes=64)
-            nc.sync.dma_start(out=raw[:], in_=wz[e, s * PASS : (s + 1) * PASS, :].rearrange("(p j) c -> p (j c)", j=4))
-            raws[e, s] = raw
+            raw = stream.tile([P, PACK * H], F32, name="wz_raw", bufs=E * Z_PASSES, align_bytes=64)
+            nc.sync.dma_start(out=raw[:], in_=wz[e, s * PASS : (s + 1) * PASS, :].rearrange("(p j) c -> p (j c)", j=PACK))
+            wz_raw[e, s] = raw
 
-        def load_codes(codes, words, experts):
+        nc.sync.dma_start(out=text_list[:], in_=offs)
+        nc.sync.dma_start(out=x_table[:], in_=x_words[0].rearrange("p t d -> p (t d)").bitcast(I32))
+        for r in range(4):
+            nc.sync.dma_start(out=x_scale_table[r:P:32, :].bitcast(I32), in_=x_scales[0, r:16:4, :].bitcast(I32))
+        load_weight_scales(w1_plane, w1_scales)
+        nc.sync.dma_start(out=patch_list[:], in_=offs2)
+        load_patch_words(0)
+        load_weight_codes(w1_codes, w1_words, 0, EARLY)
+        load_patch_words(1)
+        for q in range(4):
             nc.sync.dma_start(
-                out=codes[:, experts, :].bitcast(I32), in_=words[experts, 0].rearrange("e p n -> p e n").bitcast(I32)
+                out=z_scale_table[32 * q : 32 * q + 4 * Z_PASSES, :Q].bitcast(I32),
+                in_=z_scales[:, 4 * q : 4 * q + 4, :].bitcast(I32),
             )
-
-        def ld(what):
-            if what == "o":
-                nc.sync.dma_start(out=text_list[:], in_=offs)
-            elif what == "xw":
-                nc.sync.dma_start(out=x_table[:], in_=x_words[0].rearrange("p t d -> p (t d)").bitcast(I32))
-            elif what == "xs":
-                for r in range(4):
-                    nc.sync.dma_start(out=x_scale_table[r:P:32, :].bitcast(I32), in_=x_scales[0, r:16:4, :].bitcast(I32))
-            elif what == "o2":
-                nc.sync.dma_start(out=patch_list[:], in_=offs2)
-            elif what in ("z0", "z1"):
-                s = int(what[1])
-                nc.sync.dma_start(out=z_tables[s][:, :Q], in_=z_words[s].rearrange("p t d -> p (t d)").bitcast(I32))
-            elif what == "zs":
-                for q in range(4):
-                    nc.sync.dma_start(
-                        out=z_scale_table[32 * q : 32 * q + 4 * Z_PASSES, :Q].bitcast(I32),
-                        in_=z_scales[:, 4 * q : 4 * q + 4, :].bitcast(I32),
-                    )
-            elif what == "w1s":
-                load_weight_scales(w1_plane, w1_scales, slice(0, E))
-            elif what[0] == "A":
-                load_weight_scales(w1_plane, w1_scales, slice(int(what[1]), int(what[2])))
-            elif what[0] == "B":
-                load_weight_scales(w2_plane, w2_scales, slice(int(what[1]), int(what[2])))
-            elif what == "w2s":
-                load_weight_scales(w2_plane, w2_scales, slice(0, E))
-            elif what[0] == "a":
-                load_codes(w1_codes, w1_words, slice(int(what[1]), int(what[2])))
-            elif what[0] == "b":
-                load_codes(w2_codes, w2_words, slice(int(what[1]), int(what[2])))
-            elif what[0] == "g":
-                cols = slice(int(what[1]) * C, int(what[2]) * C)
-                nc.sync.dma_start(out=gates[TEXT][:, cols], in_=gate1[:, cols])
-            elif what[0] == "h":
-                cols = slice(int(what[1]) * C, int(what[2]) * C)
-                nc.sync.dma_start(out=gates[PATCH][:, cols], in_=gate2[:, cols])
-            else:
-                load_wz(int(what[0]), int(what[1]))
-
-        for what in ORDER.split():
-            ld(what)
-
-        for lo, hi in XCUT:
-            offsets = text_list[:, lo * C // 16 : hi * C // 16]
-            nc.vector.tensor_copy(x_slots[:, lo * C : hi * C], x_table[:].bitcast(U32).indirect(offsets))
-            nc.vector.tensor_copy(x_slot_scales[:, lo * C : hi * C], x_scale_table[:].indirect(offsets))
-
-        def gather_patches():
+        load_weight_scales(w2_plane, w2_scales)
+        load_weight_codes(w2_codes, w2_words, 0, 1)
+        load_gates(TEXT, 0, EARLY)
+        load_weight_codes(w1_codes, w1_words, EARLY, E)
+        load_weight_codes(w2_codes, w2_words, 1, EARLY)
+        load_wz(0, 0)
+        load_weight_codes(w2_codes, w2_words, EARLY, E)
+        load_wz(0, 1)
+        load_gates(TEXT, EARLY, E)
+        for e in range(1, E):
+            if e == E // 2:
+                load_gates(PATCH, 0, E)
             for s in range(Z_PASSES):
-                nc.vector.tensor_copy(z_slots[:, s, :], z_tables[s][:].bitcast(U32).indirect(patch_list[:]))
-            nc.vector.tensor_copy(z_slot_scales[:], z_scale_table[:].indirect(patch_list[:]))
-
-        for b in range(BLOCKS):
-            if b < VZ:
-                nc.vector.memset(results[TEXT][b][:], 0.0)
-            else:
-                nc.scalar.copy(results[TEXT][b][:], results[TEXT][0][:])
-
-        casted = {}
-        wz_quantised = {}
-        rows_of = {}
-        hidden = {}
-        sums_of = {}
-
-        def cast(e, s):
-            if s == 0:
-                casted[e] = stream.tile([P, Z_PASSES, H, 4], BF16, name="grouped", bufs=GRB, align_bytes=64)
-            if (e, s) not in raws:
                 load_wz(e, s)
-            nc.scalar.activation(
-                casted[e][:, s].rearrange("p (t m) j -> p m j t", t=4),
-                raws[e, s][:].rearrange("p (j m t) -> p m j t", j=4, t=4),
-                ACT.Copy,
-            )
 
-        def quantise_wz(e, passes):
-            if passes.start == 0:
-                wz_quantised[e] = (
-                    stream.tile([P, Z_PASSES * H], U32, name="wz_codes", bufs=QB, align_bytes=64),
-                    stream.tile([P, Z_PASSES * H], U8, name="wz_plane", bufs=QB, align_bytes=64),
-                )
-            codes, plane = wz_quantised[e]
-            cols = slice(passes.start * H, passes.stop * H)
-            nc.vector.quantize_mx(
-                out=codes[:, cols].bitcast(FP8X4),
-                scales=plane[:, cols],
-                in_=casted[e][:, passes].rearrange("p s c j -> p (s c j)"),
-            )
+        nc.vector.tensor_copy(x_slots[:], x_table[:].bitcast(U32).indirect(text_list[:]))
+        nc.vector.tensor_copy(x_slot_scales[:], x_scale_table[:].indirect(text_list[:]))
 
-        def first_layer(bank, modality, e):
+        nc.vector.memset(results[TEXT][0][:], 0.0)
+        for b in range(1, BLOCKS):
+            nc.scalar.copy(results[TEXT][b][:], results[TEXT][0][:])
+
+        for s in range(Z_PASSES):
+            nc.vector.tensor_copy(z_slots[:, s, :], z_tables[s][:].bitcast(U32).indirect(patch_list[:]))
+        nc.vector.tensor_copy(z_slot_scales[:], z_scale_table[:].indirect(patch_list[:]))
+
+        wz_cast = {}
+        wz_mx = {}
+        hidden_mx = {}
+
+        def quantise_hidden(modality, e, values, bufs):
+            codes = stream.tile([P, C], U32, name="hidden_codes%d" % modality, bufs=bufs, align_bytes=64)
+            plane = stream.tile([P, C], U8, name="hidden_plane%d" % modality, bufs=bufs, align_bytes=64)
+            nc.vector.quantize_mx(out=codes[:].bitcast(FP8X4), scales=plane[:], in_=values)
+            hidden_mx[modality, e] = (codes, plane)
+
+        def text_hidden(e):
+            bank = text_banks[e % len(text_banks)]
             slots = slice(e * C, (e + 1) * C)
-            if modality == TEXT:
-                nc.tensor.matmul_mx(
-                    out=bank[:],
-                    lhsT=x_slots[:, slots].bitcast(FP8X4),
-                    lhsT_scale=x_slot_scales[:, slots],
-                    rhs=w1_codes[:, e, :].bitcast(FP4X4),
-                    rhs_scale=w1_plane[:, e, :],
-                    start=True,
-                    stop=True,
-                )
-            else:
-                codes, plane = wz_quantised[e]
-                for s in range(Z_PASSES):
-                    cols = slice(s * H, (s + 1) * H)
-                    nc.tensor.matmul_mx(
-                        out=bank[:],
-                        lhsT=z_slots[:, s, slots].bitcast(FP8X4),
-                        lhsT_scale=z_slot_scales[4 * s :, slots],
-                        rhs=codes[:, cols].bitcast(FP8X4),
-                        rhs_scale=plane[:, cols],
-                        start=(s == 0),
-                        stop=(s == Z_PASSES - 1),
-                    )
-            rows = stream.tile([P, H], BF16, name="rows%d" % modality, bufs=2, align_bytes=64)
+            nc.tensor.matmul_mx(
+                out=bank[:],
+                lhsT=x_slots[:, slots].bitcast(FP8X4),
+                lhsT_scale=x_slot_scales[:, slots],
+                rhs=w1_codes[:, e, :].bitcast(FP4X4),
+                rhs_scale=w1_plane[:, e, :],
+                start=True,
+                stop=True,
+            )
+            rows = stream.tile([P, H], BF16, name="text_rows", bufs=2, align_bytes=64)
             nc.scalar.activation(
                 rows[:].rearrange("s (u p d) -> s u p d", u=2, d=2),
                 bank[:].rearrange("s (p u d) -> s u p d", u=2, d=2),
                 ACT.Relu,
             )
-            rows_of[modality, e] = rows
+            pairs = rows[:].bitcast(F32)
+            for u in range(2):
+                nc.tensor.transpose(bank[:, u * C : (u + 1) * C], pairs[:, u * P : (u + 1) * P], identity[:])
+            turned = stream.tile([P, PACK * C], BF16, name="text_turned", bufs=4, align_bytes=64)
+            nc.scalar.copy(
+                turned[:].bitcast(F32).rearrange("p (s u) -> p s u", u=2),
+                bank[:, : 2 * C].rearrange("p (u s) -> p s u", u=2),
+            )
+            quantise_hidden(TEXT, e, turned[:], E)
 
-        def patch_hidden(bank, e, room):
+        def cast_wz(e, s):
+            if s == 0:
+                wz_cast[e] = stream.tile([P, Z_PASSES, H, PACK], BF16, name="wz_cast", bufs=3, align_bytes=64)
+            nc.scalar.copy(
+                wz_cast[e][:, s].rearrange("p (g h m) j -> p g m j h", g=2, h=2),
+                wz_raw[e, s][:].rearrange("p (j m g h) -> p g m j h", j=PACK, g=2, h=2),
+            )
+
+        def quantise_wz(e, first, last):
+            if first == 0:
+                wz_mx[e] = (
+                    stream.tile([P, Z_PASSES * H], U32, name="wz_codes", bufs=3, align_bytes=64),
+                    stream.tile([P, Z_PASSES * H], U8, name="wz_plane", bufs=3, align_bytes=64),
+                )
+            codes, plane = wz_mx[e]
+            cols = slice(first * H, last * H)
+            nc.vector.quantize_mx(
+                out=codes[:, cols].bitcast(FP8X4),
+                scales=plane[:, cols],
+                in_=wz_cast[e][:, first:last].rearrange("p s c j -> p (s c j)"),
+            )
+
+        def patch_hidden(e, spent):
+            bank = patch_banks[e % len(patch_banks)]
             slots = slice(e * C, (e + 1) * C)
-            codes, plane = wz_quantised[e]
-            for t in range(4):
+            codes, plane = wz_mx[e]
+            for t in range(PACK):
                 for s in range(Z_PASSES):
                     cols = slice(s * H + t * P, s * H + (t + 1) * P)
                     nc.tensor.matmul_mx(
@@ -236,33 +216,14 @@ def tile_moe_mmo_relu_kernel(
                         start=(s == 0),
                         stop=(s == Z_PASSES - 1),
                     )
-            if room is None:
-                room = stream.tile([P, 4 * H], F32, name="room", bufs=2, align_bytes=64)
-            values = room[:, : 2 * C].bitcast(BF16)
+            values = spent[:, : 2 * C].bitcast(BF16)
             nc.scalar.activation(
-                values.rearrange("p (c t) -> p c t", t=4), bank[:].rearrange("p (t c) -> p c t", t=4), ACT.Relu
+                values.rearrange("p (c t) -> p c t", t=PACK), bank[:].rearrange("p (t c) -> p c t", t=PACK), ACT.Relu
             )
-            codes = stream.tile([P, C], U32, name="hidden_codes1", bufs=HB, align_bytes=64)
-            plane = stream.tile([P, C], U8, name="hidden_plane1", bufs=HB, align_bytes=64)
-            nc.vector.quantize_mx(out=codes[:].bitcast(FP8X4), scales=plane[:], in_=values)
-            hidden[PATCH, e] = (codes, plane)
+            quantise_hidden(PATCH, e, values, 3)
 
-        def turn(bank, modality, e):
-            pairs = rows_of[modality, e][:].bitcast(F32)
-            for u in range(2):
-                nc.tensor.transpose(bank[:, u * C : (u + 1) * C], pairs[:, u * P : (u + 1) * P], identity[:])
-            turned = stream.tile([P, 4 * C], BF16, name="turned%d" % modality, bufs=TNB, align_bytes=64)
-            nc.scalar.copy(
-                turned[:].bitcast(F32).rearrange("p (s u) -> p s u", u=2),
-                bank[:, : 2 * C].rearrange("p (u s) -> p s u", u=2),
-            )
-            codes = stream.tile([P, C], U32, name="hidden_codes%d" % modality, bufs=E, align_bytes=64)
-            plane = stream.tile([P, C], U8, name="hidden_plane%d" % modality, bufs=E, align_bytes=64)
-            nc.vector.quantize_mx(out=codes[:].bitcast(FP8X4), scales=plane[:], in_=turned[:])
-            hidden[modality, e] = (codes, plane)
-
-        def second_layer(bank, modality, e, blocks, room, part):
-            codes, plane = hidden[modality, e]
+        def deliver(modality, e, bank, sums, blocks=range(BLOCKS)):
+            codes, plane = hidden_mx[modality, e]
             for b in blocks:
                 nc.tensor.matmul_mx(
                     out=bank[:, b * C : (b + 1) * C],
@@ -273,14 +234,9 @@ def tile_moe_mmo_relu_kernel(
                     start=True,
                     stop=True,
                 )
-            if room is None:
-                room = stream.tile([P, BLOCKS * C], F32, name="sums", bufs=SB)
-                sums = room[:]
-            else:
-                sums = room[:, part * H : (part + 1) * H]
             cols = slice(blocks.start * C, blocks.stop * C)
             nc.scalar.copy(sums[:, cols], bank[:, cols])
-            offsets = lists[modality][:, e * C // 16 : (e + 1) * C // 16]
+            offsets = lists[modality][:, e * LIST_COLS : (e + 1) * LIST_COLS]
             for b in blocks:
                 nc.vector.tensor_tensor(
                     results[modality][b][:].indirect(offsets),
@@ -293,21 +249,56 @@ def tile_moe_mmo_relu_kernel(
                     width = (T, Q)[modality]
                     nc.sync.dma_start(out=out[b * P : (b + 1) * P, first : first + width], in_=results[modality][b][:])
 
-        for step in PROGRAM.split():
-            parts = step.split("@")
-            room = raws[int(parts[1][0]), int(parts[1][1])] if len(parts) > 1 else None
-            kind, args = step[0], [int(c) for c in parts[0][1:]]
-            if kind == "Z":
-                gather_patches()
-            elif kind == "c":
-                cast(args[0], args[1])
-            elif kind == "q":
-                quantise_wz(args[0], slice(args[1], args[2]))
-            elif kind == "f":
-                first_layer(banks[args[0]], args[1], args[2])
-            elif kind == "t":
-                turn(banks[args[0]], args[1], args[2])
-            elif kind == "p":
-                patch_hidden(banks[args[0]], args[1], room)
-            elif kind == "s":
-                second_layer(banks[args[0]], args[1], args[2], range(args[3], args[4]), room, int(parts[1][2]) if len(parts) > 1 and len(parts[1]) > 2 else 1 + args[1])
+        def fresh_sums():
+            sums = stream.tile([P, BLOCKS * C], F32, name="sums", bufs=2)
+            return sums[:]
+
+        def quarter(e, s, part):
+            return wz_raw[e, s][:, part * H : (part + 1) * H]
+
+        for e in range(EARLY):
+            text_hidden(e)
+        deliver(TEXT, 0, result_banks[0], fresh_sums())
+        text_hidden(3)
+        deliver(TEXT, 1, result_banks[1], fresh_sums())
+        text_hidden(4)
+        text_hidden(5)
+
+        cast_wz(0, 0)
+        deliver(TEXT, 2, result_banks[0], quarter(0, 0, 1))
+        cast_wz(0, 1)
+        quantise_wz(0, 0, 2)
+        deliver(TEXT, 3, result_banks[1], quarter(0, 1, 1))
+        cast_wz(1, 0)
+        deliver(TEXT, 4, result_banks[0], quarter(0, 1, 3))
+        cast_wz(1, 1)
+        quantise_wz(1, 0, 2)
+        patch_hidden(0, wz_raw[1, 0])
+        deliver(TEXT, 5, result_banks[1], quarter(1, 0, 1))
+
+        for e in (2, 3):
+            cast_wz(e, 0)
+            cast_wz(e, 1)
+            quantise_wz(e, 0, 2)
+            patch_hidden(e - 1, wz_raw[e, 0])
+            deliver(PATCH, e - 2, result_banks[e % 2], quarter(e, 0, 2))
+
+        cast_wz(4, 0)
+        patch_hidden(3, wz_raw[3, 1])
+        deliver(PATCH, 2, result_banks[0], quarter(3, 1, 2))
+        cast_wz(4, 1)
+        quantise_wz(4, 0, 2)
+        deliver(PATCH, 3, result_banks[1], quarter(4, 0, 2))
+        cast_wz(5, 0)
+        quantise_wz(5, 0, 1)
+        patch_hidden(4, wz_raw[4, 1])
+        cast_wz(5, 1)
+        quantise_wz(5, 1, 2)
+
+        deliver(PATCH, 4, result_banks[0], quarter(5, 0, 2), range(0, 1))
+        deliver(PATCH, 4, text_banks[0], quarter(5, 0, 2), range(1, BLOCKS - 1))
+        patch_hidden(5, wz_raw[4, 0])
+        deliver(PATCH, 4, patch_banks[1], quarter(5, 0, 2), range(BLOCKS - 1, BLOCKS))
+        last_sums = fresh_sums()
+        deliver(PATCH, 5, result_banks[1], last_sums, range(0, 1))
+        deliver(PATCH, 5, result_banks[0], last_sums, range(1, BLOCKS))

@@ -102,20 +102,20 @@ def tile_moe_mmo_relu_kernel(
 
         nc.sync.dma_start(out=text_list[:], in_=offs)
         nc.sync.dma_start(out=x_table[:], in_=x_words[0].rearrange("p t d -> p (t d)").bitcast(I32))
+        nc.sync.dma_start(out=patch_list[:], in_=offs2)
         for r in range(4):
             nc.sync.dma_start(out=x_scale_table[r:P:32, :].bitcast(I32), in_=x_scales[0, r:16:4, :].bitcast(I32))
         load_weight_scales(w1_plane, w1_scales)
-        nc.sync.dma_start(out=patch_list[:], in_=offs2)
-        load_patch_words(0)
-        load_weight_codes(w1_codes, w1_words, 0, EARLY)
-        load_patch_words(1)
         for q in range(4):
             nc.sync.dma_start(
                 out=z_scale_table[32 * q : 32 * q + 4 * Z_PASSES, :Q].bitcast(I32),
                 in_=z_scales[:, 4 * q : 4 * q + 4, :].bitcast(I32),
             )
         load_weight_scales(w2_plane, w2_scales)
+        load_weight_codes(w1_codes, w1_words, 0, EARLY)
+        load_patch_words(0)
         load_weight_codes(w2_codes, w2_words, 0, 1)
+        load_patch_words(1)
         load_gates(TEXT, 0, EARLY)
         load_weight_codes(w1_codes, w1_words, EARLY, E)
         load_weight_codes(w2_codes, w2_words, 1, EARLY)
@@ -222,83 +222,85 @@ def tile_moe_mmo_relu_kernel(
             )
             quantise_hidden(PATCH, e, values, 3)
 
-        def deliver(modality, e, bank, sums, blocks=range(BLOCKS)):
-            codes, plane = hidden_mx[modality, e]
-            for b in blocks:
-                nc.tensor.matmul_mx(
-                    out=bank[:, b * C : (b + 1) * C],
-                    lhsT=w2_codes[:, e, 2 * b * P : 2 * (b + 1) * P].bitcast(FP4X4),
-                    lhsT_scale=w2_plane[:, e, b * P : (b + 1) * P],
-                    rhs=codes[:].bitcast(FP8X4),
-                    rhs_scale=plane[:],
-                    start=True,
-                    stop=True,
+        def deliver(modality, experts, banks, sums, blocks=range(BLOCKS)):
+            sums = sums.rearrange("p (b c) -> p b c", b=BLOCKS)
+            rows = slice(blocks.start, blocks.stop)
+            for place, (e, bank) in enumerate(zip(experts, banks)):
+                codes, plane = hidden_mx[modality, e]
+                for b in blocks:
+                    nc.tensor.matmul_mx(
+                        out=bank[:, b * C : (b + 1) * C],
+                        lhsT=w2_codes[:, e, 2 * b * P : 2 * (b + 1) * P].bitcast(FP4X4),
+                        lhsT_scale=w2_plane[:, e, b * P : (b + 1) * P],
+                        rhs=codes[:].bitcast(FP8X4),
+                        rhs_scale=plane[:],
+                        start=True,
+                        stop=True,
+                    )
+                nc.scalar.copy(
+                    sums[:, rows, place * C : (place + 1) * C], bank[:].rearrange("p (b c) -> p b c", b=BLOCKS)[:, rows, :]
                 )
-            cols = slice(blocks.start * C, blocks.stop * C)
-            nc.scalar.copy(sums[:, cols], bank[:, cols])
-            offsets = lists[modality][:, e * LIST_COLS : (e + 1) * LIST_COLS]
+            offsets = lists[modality][:, experts.start * LIST_COLS : experts.stop * LIST_COLS]
             for b in blocks:
                 nc.vector.tensor_tensor(
                     results[modality][b][:].indirect(offsets),
-                    sums[:, b * C : (b + 1) * C],
-                    gates[modality][:, e * C : (e + 1) * C],
+                    sums[:, b, :],
+                    gates[modality][:, experts.start * C : experts.stop * C],
                     MULT,
                 )
-                if e == E - 1:
+                if experts.stop == E:
                     first = modality * T
                     width = (T, Q)[modality]
                     nc.sync.dma_start(out=out[b * P : (b + 1) * P, first : first + width], in_=results[modality][b][:])
 
-        def fresh_sums():
-            sums = stream.tile([P, BLOCKS * C], F32, name="sums", bufs=2)
+        def fresh_sums(experts):
+            sums = stream.tile([P, experts * BLOCKS * C], F32, name="sums", bufs=2)
             return sums[:]
 
-        def quarter(e, s, part):
-            return wz_raw[e, s][:, part * H : (part + 1) * H]
+        def quarters(e, s, first, last):
+            return wz_raw[e, s][:, first * H : last * H]
 
         for e in range(EARLY):
             text_hidden(e)
-        deliver(TEXT, 0, result_banks[0], fresh_sums())
+        deliver(TEXT, range(0, 1), [result_banks[0]], fresh_sums(1))
         text_hidden(3)
-        deliver(TEXT, 1, result_banks[1], fresh_sums())
         text_hidden(4)
+        deliver(TEXT, range(1, 3), [result_banks[1], text_banks[0]], fresh_sums(2))
         text_hidden(5)
 
         cast_wz(0, 0)
-        deliver(TEXT, 2, result_banks[0], quarter(0, 0, 1))
         cast_wz(0, 1)
         quantise_wz(0, 0, 2)
-        deliver(TEXT, 3, result_banks[1], quarter(0, 1, 1))
+        deliver(TEXT, range(3, 5), result_banks, quarters(0, 1, 1, 3))
         cast_wz(1, 0)
-        deliver(TEXT, 4, result_banks[0], quarter(0, 1, 3))
         cast_wz(1, 1)
         quantise_wz(1, 0, 2)
         patch_hidden(0, wz_raw[1, 0])
-        deliver(TEXT, 5, result_banks[1], quarter(1, 0, 1))
+        deliver(TEXT, range(5, 6), [result_banks[1]], quarters(1, 0, 1, 2))
 
         for e in (2, 3):
             cast_wz(e, 0)
             cast_wz(e, 1)
             quantise_wz(e, 0, 2)
             patch_hidden(e - 1, wz_raw[e, 0])
-            deliver(PATCH, e - 2, result_banks[e % 2], quarter(e, 0, 2))
+            deliver(PATCH, range(e - 2, e - 1), [result_banks[e % 2]], quarters(e, 0, 2, 3))
 
         cast_wz(4, 0)
         patch_hidden(3, wz_raw[3, 1])
-        deliver(PATCH, 2, result_banks[0], quarter(3, 1, 2))
+        deliver(PATCH, range(2, 3), [result_banks[0]], quarters(3, 1, 2, 3))
         cast_wz(4, 1)
         quantise_wz(4, 0, 2)
-        deliver(PATCH, 3, result_banks[1], quarter(4, 0, 2))
+        deliver(PATCH, range(3, 4), [result_banks[1]], quarters(4, 0, 2, 3))
         cast_wz(5, 0)
         quantise_wz(5, 0, 1)
         patch_hidden(4, wz_raw[4, 1])
         cast_wz(5, 1)
         quantise_wz(5, 1, 2)
 
-        deliver(PATCH, 4, result_banks[0], quarter(5, 0, 2), range(0, 1))
-        deliver(PATCH, 4, text_banks[0], quarter(5, 0, 2), range(1, BLOCKS - 1))
+        deliver(PATCH, range(4, 5), [result_banks[0]], quarters(5, 0, 2, 3), range(0, 1))
+        deliver(PATCH, range(4, 5), [text_banks[0]], quarters(5, 0, 2, 3), range(1, BLOCKS - 1))
         patch_hidden(5, wz_raw[4, 0])
-        deliver(PATCH, 4, patch_banks[1], quarter(5, 0, 2), range(BLOCKS - 1, BLOCKS))
-        last_sums = fresh_sums()
-        deliver(PATCH, 5, result_banks[1], last_sums, range(0, 1))
-        deliver(PATCH, 5, result_banks[0], last_sums, range(1, BLOCKS))
+        deliver(PATCH, range(4, 5), [patch_banks[1]], quarters(5, 0, 2, 3), range(BLOCKS - 1, BLOCKS))
+        last_sums = fresh_sums(1)
+        deliver(PATCH, range(5, 6), [result_banks[1]], last_sums, range(0, 1))
+        deliver(PATCH, range(5, 6), [result_banks[0]], last_sums, range(1, BLOCKS))

from contextlib import ExitStack

import concourse.mybir as mybir
from concourse.masks import make_identity

K, L, T, Q, E, C = 512, 1024, 1024, 768, 6, 128
H, N = 512, 512
SLOTS = E * C
FLOPS = 2 * SLOTS * (K * H + L * H + 2 * H * N)

F32 = mybir.dt.float32
BF16 = mybir.dt.bfloat16
I32 = mybir.dt.int32
U32 = mybir.dt.uint32
U16 = mybir.dt.uint16
U8 = mybir.dt.uint8
FP8X4 = mybir.dt.float8_e4m3fn_x4
FP4X4 = mybir.dt.float4_e2m1fn_x4
ACT = mybir.ActivationFunctionType
MULT = mybir.AluOpType.mult

P = 128
PACK = 4
PASS = P * PACK
Z_PASSES = L // PASS
BLOCKS = N // P
LIST_COLS = C // 16
Z_WINDOW = 1024
EARLY = 3
TEXT, PATCH = 0, 1


def tile_moe_mmo_relu_kernel(
    tc, x_words, x_scales, z_words, z_scales, w1_words, w1_scales, wz, w2_words, w2_scales, gate1, gate2, offs, offs2, out
):
    nc = tc.nc
    with ExitStack() as ctx:
        held = ctx.enter_context(tc.tile_pool(name="held", bufs=1))
        stream = ctx.enter_context(tc.tile_pool(name="stream", bufs=1))
        psum = ctx.enter_context(tc.psum_pool(name="psum", bufs=1))

        text_list = held.tile([P, SLOTS // 16], U16, name="text_list")
        patch_list = held.tile([P, SLOTS // 16], U16, name="patch_list")
        x_table = held.tile([P, T], I32, name="x_table", align_bytes=64)
        x_scale_table = held.tile([P, T], U8, name="x_scale_table", align_bytes=64)
        z_tables = [held.tile([P, Z_WINDOW], I32, name="z_table%d" % s, align_bytes=64) for s in range(Z_PASSES)]
        z_scale_table = held.tile([P, Z_WINDOW], U8, name="z_scale_table", align_bytes=64)
        x_slots = held.tile([P, SLOTS], U32, name="x_slots", align_bytes=64)
        x_slot_scales = held.tile([P, SLOTS], U8, name="x_slot_scales", align_bytes=64)
        z_slots = held.tile([P, Z_PASSES, SLOTS], U32, name="z_slots", align_bytes=64)
        z_slot_scales = held.tile([P, SLOTS], U8, name="z_slot_scales", align_bytes=64)
        w1_codes = held.tile([P, E, 2 * H], U8, name="w1_codes", align_bytes=64)
        w1_plane = held.tile([P, E, H], U8, name="w1_plane", align_bytes=64)
        w2_codes = held.tile([P, E, 2 * N], U8, name="w2_codes", align_bytes=64)
        w2_plane = held.tile([P, E, N], U8, name="w2_plane", align_bytes=64)
        gates = [held.tile([P, SLOTS], F32, name="gate%d" % m) for m in (TEXT, PATCH)]
        identity = held.tile([P, P], F32, name="identity")
        results = [
            [held.tile([P, width], F32, name="result%d_%d" % (m, b)) for b in range(BLOCKS)]
            for m, width in ((TEXT, T), (PATCH, Q))
        ]
        lists = (text_list, patch_list)

        text_banks = [psum.tile([P, H], F32, name="text_bank%d" % i) for i in range(3)]
        result_banks = [psum.tile([P, BLOCKS * C], F32, name="result_bank%d" % i) for i in range(2)]
        patch_banks = [psum.tile([P, PACK * C], F32, name="patch_bank%d" % i) for i in range(2)]

        nc.vector.memset(x_scale_table[:].bitcast(I32), 0)
        nc.vector.memset(w1_plane[:].rearrange("p e n -> p (e n)").bitcast(I32), 0)
        nc.vector.memset(z_scale_table[:].bitcast(I32), 0)
        nc.vector.memset(w2_plane[:].rearrange("p e n -> p (e n)").bitcast(I32), 0)
        for s in range(Z_PASSES):
            nc.vector.memset(z_tables[s][:, Q:], 0)
        make_identity(nc, identity[:])

        def load_weight_scales(plane, scales):
            for r in range(4):
                nc.sync.dma_start(
                    out=plane[r:P:32, :, :].bitcast(I32),
                    in_=scales[:, 0, r:16:4, :].rearrange("e q n -> q e n").bitcast(I32),
                )

        def load_weight_codes(codes, words, first, last):
            nc.sync.dma_start(
                out=codes[:, first:last, :].bitcast(I32),
                in_=words[first:last, 0].rearrange("e p n -> p e n").bitcast(I32),
            )

        def load_patch_words(s):
            nc.sync.dma_start(out=z_tables[s][:, :Q], in_=z_words[s].rearrange("p t d -> p (t d)").bitcast(I32))

        def load_gates(modality, first, last):
            cols = slice(first * C, last * C)
            nc.sync.dma_start(out=gates[modality][:, cols], in_=(gate1, gate2)[modality][:, cols])

        wz_raw = {}

        def load_wz(e, s):
            raw = stream.tile([P, PACK * H], F32, name="wz_raw", bufs=E * Z_PASSES, align_bytes=64)
            nc.sync.dma_start(out=raw[:], in_=wz[e, s * PASS : (s + 1) * PASS, :].rearrange("(p j) c -> p (j c)", j=PACK))
            wz_raw[e, s] = raw

        nc.sync.dma_start(out=text_list[:], in_=offs)
        nc.sync.dma_start(out=x_table[:], in_=x_words[0].rearrange("p t d -> p (t d)").bitcast(I32))
        nc.sync.dma_start(out=patch_list[:], in_=offs2)
        for r in range(4):
            nc.sync.dma_start(out=x_scale_table[r:P:32, :].bitcast(I32), in_=x_scales[0, r:16:4, :].bitcast(I32))
        load_weight_scales(w1_plane, w1_scales)
        for q in range(4):
            nc.sync.dma_start(
                out=z_scale_table[32 * q : 32 * q + 4 * Z_PASSES, :Q].bitcast(I32),
                in_=z_scales[:, 4 * q : 4 * q + 4, :].bitcast(I32),
            )
        load_weight_scales(w2_plane, w2_scales)
        load_weight_codes(w1_codes, w1_words, 0, EARLY)
        load_patch_words(0)
        load_weight_codes(w2_codes, w2_words, 0, 1)
        load_patch_words(1)
        load_gates(TEXT, 0, EARLY)
        load_weight_codes(w1_codes, w1_words, EARLY, E)
        load_weight_codes(w2_codes, w2_words, 1, EARLY)
        load_wz(0, 0)
        load_weight_codes(w2_codes, w2_words, EARLY, E)
        load_wz(0, 1)
        load_gates(TEXT, EARLY, E)
        for e in range(1, E):
            if e == E // 2:
                load_gates(PATCH, 0, E)
            for s in range(Z_PASSES):
                load_wz(e, s)

        nc.vector.tensor_copy(x_slots[:], x_table[:].bitcast(U32).indirect(text_list[:]))
        nc.vector.tensor_copy(x_slot_scales[:], x_scale_table[:].indirect(text_list[:]))

        nc.vector.memset(results[TEXT][0][:], 0.0)
        for b in range(1, BLOCKS):
            nc.scalar.copy(results[TEXT][b][:], results[TEXT][0][:])

        for s in range(Z_PASSES):
            nc.vector.tensor_copy(z_slots[:, s, :], z_tables[s][:].bitcast(U32).indirect(patch_list[:]))
        nc.vector.tensor_copy(z_slot_scales[:], z_scale_table[:].indirect(patch_list[:]))

        wz_cast = {}
        wz_mx = {}
        hidden_mx = {}

        def quantise_hidden(modality, e, values, bufs):
            codes = stream.tile([P, C], U32, name="hidden_codes%d" % modality, bufs=bufs, align_bytes=64)
            plane = stream.tile([P, C], U8, name="hidden_plane%d" % modality, bufs=bufs, align_bytes=64)
            nc.vector.quantize_mx(out=codes[:].bitcast(FP8X4), scales=plane[:], in_=values)
            hidden_mx[modality, e] = (codes, plane)

        def text_hidden(e):
            bank = text_banks[e % len(text_banks)]
            slots = slice(e * C, (e + 1) * C)
            nc.tensor.matmul_mx(
                out=bank[:],
                lhsT=x_slots[:, slots].bitcast(FP8X4),
                lhsT_scale=x_slot_scales[:, slots],
                rhs=w1_codes[:, e, :].bitcast(FP4X4),
                rhs_scale=w1_plane[:, e, :],
                start=True,
                stop=True,
            )
            rows = stream.tile([P, H], BF16, name="text_rows", bufs=2, align_bytes=64)
            nc.scalar.activation(
                rows[:].rearrange("s (u p d) -> s u p d", u=2, d=2),
                bank[:].rearrange("s (p u d) -> s u p d", u=2, d=2),
                ACT.Relu,
            )
            pairs = rows[:].bitcast(F32)
            for u in range(2):
                nc.tensor.transpose(bank[:, u * C : (u + 1) * C], pairs[:, u * P : (u + 1) * P], identity[:])
            turned = stream.tile([P, PACK * C], BF16, name="text_turned", bufs=4, align_bytes=64)
            nc.scalar.copy(
                turned[:].bitcast(F32).rearrange("p (s u) -> p s u", u=2),
                bank[:, : 2 * C].rearrange("p (u s) -> p s u", u=2),
            )
            quantise_hidden(TEXT, e, turned[:], E)

        def cast_wz(e, s):
            if s == 0:
                wz_cast[e] = stream.tile([P, Z_PASSES, H, PACK], BF16, name="wz_cast", bufs=3, align_bytes=64)
            nc.scalar.copy(
                wz_cast[e][:, s].rearrange("p (g h m) j -> p g m j h", g=2, h=2),
                wz_raw[e, s][:].rearrange("p (j m g h) -> p g m j h", j=PACK, g=2, h=2),
            )

        def quantise_wz(e, first, last):
            if first == 0:
                wz_mx[e] = (
                    stream.tile([P, Z_PASSES * H], U32, name="wz_codes", bufs=3, align_bytes=64),
                    stream.tile([P, Z_PASSES * H], U8, name="wz_plane", bufs=3, align_bytes=64),
                )
            codes, plane = wz_mx[e]
            cols = slice(first * H, last * H)
            nc.vector.quantize_mx(
                out=codes[:, cols].bitcast(FP8X4),
                scales=plane[:, cols],
                in_=wz_cast[e][:, first:last].rearrange("p s c j -> p (s c j)"),
            )

        def patch_hidden(e, spent):
            bank = patch_banks[e % len(patch_banks)]
            slots = slice(e * C, (e + 1) * C)
            codes, plane = wz_mx[e]
            for t in range(PACK):
                for s in range(Z_PASSES):
                    cols = slice(s * H + t * P, s * H + (t + 1) * P)
                    nc.tensor.matmul_mx(
                        out=bank[:, t * C : (t + 1) * C],
                        lhsT=codes[:, cols].bitcast(FP8X4),
                        lhsT_scale=plane[:, cols],
                        rhs=z_slots[:, s, slots].bitcast(FP8X4),
                        rhs_scale=z_slot_scales[4 * s :, slots],
                        start=(s == 0),
                        stop=(s == Z_PASSES - 1),
                    )
            values = spent[:, : 2 * C].bitcast(BF16)
            nc.scalar.activation(
                values.rearrange("p (c t) -> p c t", t=PACK), bank[:].rearrange("p (t c) -> p c t", t=PACK), ACT.Relu
            )
            quantise_hidden(PATCH, e, values, 3)

        def deliver(modality, experts, banks, sums, blocks=range(BLOCKS)):
            sums = sums.rearrange("p (b c) -> p b c", b=BLOCKS)
            rows = slice(blocks.start, blocks.stop)
            for place, (e, bank) in enumerate(zip(experts, banks)):
                codes, plane = hidden_mx[modality, e]
                for b in blocks:
                    nc.tensor.matmul_mx(
                        out=bank[:, b * C : (b + 1) * C],
                        lhsT=w2_codes[:, e, 2 * b * P : 2 * (b + 1) * P].bitcast(FP4X4),
                        lhsT_scale=w2_plane[:, e, b * P : (b + 1) * P],
                        rhs=codes[:].bitcast(FP8X4),
                        rhs_scale=plane[:],
                        start=True,
                        stop=True,
                    )
                nc.scalar.copy(
                    sums[:, rows, place * C : (place + 1) * C], bank[:].rearrange("p (b c) -> p b c", b=BLOCKS)[:, rows, :]
                )
            offsets = lists[modality][:, experts.start * LIST_COLS : experts.stop * LIST_COLS]
            for b in blocks:
                nc.vector.tensor_tensor(
                    results[modality][b][:].indirect(offsets),
                    sums[:, b, :],
                    gates[modality][:, experts.start * C : experts.stop * C],
                    MULT,
                )
                if experts.stop == E:
                    first = modality * T
                    width = (T, Q)[modality]
                    nc.sync.dma_start(out=out[b * P : (b + 1) * P, first : first + width], in_=results[modality][b][:])

        def fresh_sums(experts):
            sums = stream.tile([P, experts * BLOCKS * C], F32, name="sums", bufs=2)
            return sums[:]

        def quarters(e, s, first, last):
            return wz_raw[e, s][:, first * H : last * H]

        for e in range(EARLY):
            text_hidden(e)
        deliver(TEXT, range(0, 1), [result_banks[0]], fresh_sums(1))
        text_hidden(3)
        text_hidden(4)
        deliver(TEXT, range(1, 3), [result_banks[1], text_banks[0]], fresh_sums(2))
        text_hidden(5)

        cast_wz(0, 0)
        cast_wz(0, 1)
        quantise_wz(0, 0, 2)
        deliver(TEXT, range(3, 5), result_banks, quarters(0, 1, 1, 3))
        cast_wz(1, 0)
        cast_wz(1, 1)
        quantise_wz(1, 0, 2)
        patch_hidden(0, wz_raw[1, 0])
        deliver(TEXT, range(5, 6), [result_banks[1]], quarters(1, 0, 1, 2))

        for e in (2, 3):
            cast_wz(e, 0)
            cast_wz(e, 1)
            quantise_wz(e, 0, 2)
            patch_hidden(e - 1, wz_raw[e, 0])
            deliver(PATCH, range(e - 2, e - 1), [result_banks[e % 2]], quarters(e, 0, 2, 3))

        cast_wz(4, 0)
        patch_hidden(3, wz_raw[3, 1])
        deliver(PATCH, range(2, 3), [result_banks[0]], quarters(3, 1, 2, 3))
        cast_wz(4, 1)
        quantise_wz(4, 0, 2)
        deliver(PATCH, range(3, 4), [result_banks[1]], quarters(4, 0, 2, 3))
        cast_wz(5, 0)
        quantise_wz(5, 0, 1)
        patch_hidden(4, wz_raw[4, 1])
        cast_wz(5, 1)
        quantise_wz(5, 1, 2)

        deliver(PATCH, range(4, 5), [result_banks[0]], quarters(5, 0, 2, 3), range(0, 1))
        deliver(PATCH, range(4, 5), [text_banks[0]], quarters(5, 0, 2, 3), range(1, BLOCKS - 1))
        patch_hidden(5, wz_raw[4, 0])
        deliver(PATCH, range(4, 5), [patch_banks[1]], quarters(5, 0, 2, 3), range(BLOCKS - 1, BLOCKS))
        last_sums = fresh_sums(1)
        deliver(PATCH, range(5, 6), [result_banks[1]], last_sums, range(0, 1))
        deliver(PATCH, range(5, 6), [result_banks[0]], last_sums, range(1, BLOCKS))
